import numpy as np
import ml_dtypes


def mxq(x, axis, fmt="e4m3"):
    dtype, down = {"e4m3": (ml_dtypes.float8_e4m3fn, 7), "e5m2": (ml_dtypes.float8_e5m2, 14)}[fmt]
    v = np.moveaxis(np.asarray(x, np.float32).astype(ml_dtypes.bfloat16).astype(np.float64), axis, -1)
    blocks = v.reshape(v.shape[:-1] + (-1, 32))
    amax = np.abs(blocks).max(-1, keepdims=True)
    byte = np.maximum(np.where(amax > 0, np.frexp(amax)[1] - 1 + 127, 0) - down, 1)
    scale = np.exp2(byte - 127.0)
    codes = (blocks / scale).astype(np.float32).astype(dtype).astype(np.float64)
    return np.moveaxis((codes * scale).reshape(v.shape), -1, axis)


WIDE = False


def mx_kscale(k):
    if not WIDE:
        return np.ones(k)
    levels = np.array([10, -10, 5, -5, 0])
    if k % 512:
        return np.exp2(np.random.permutation(np.resize(levels, k // 32))).repeat(32)
    a = np.empty((k // 512, 16))
    for p in range(k // 512):
        a[p, :8] = np.random.permutation(np.resize(levels, 8))
        for g in range(8):
            far = levels[np.abs(levels - a[p, g]) >= 10]
            a[p, g + 8] = far[np.random.randint(len(far))]
    return np.exp2(a.ravel()).repeat(32)


def f64(x):
    return np.asarray(x).astype(np.float64)


def striped(idx):
    return np.tile(idx.reshape(-1, 16).T, (8, 1)).astype(np.uint16)


def unstriped(offs):
    return offs[:16].T.reshape(-1).astype(np.int64)


K, T, E, C, N = 1024, 2048, 4, 256, 512


def by_expert(wq, xq):
    return np.concatenate([wq[e].T @ xq[:, e * C:(e + 1) * C] for e in range(E)], axis=1)


def setup_inputs():
    n = np.random.standard_normal
    s = mx_kscale(K)[:, None]
    return {
        "xT": (n((K, T)) * s).astype(np.float32),
        "w": (n((E, K, N)) / np.sqrt(K) / s[None]).astype(np.float32),
        "gate": np.tile(np.random.uniform(0.2, 1.0, E * C), (N, 1)).astype(np.float32),
        "offs": striped(np.random.permutation(T)[:E * C]),
    }


def reference(xT, w, gate, offs):
    idx = unstriped(offs)
    xq = mxq(f64(xT)[:, idx], 0, "e4m3")
    y = by_expert(mxq(f64(w), 1, "e4m3"), xq)
    out = np.zeros((N, T))
    out[:, idx] = f64(gate) * y
    return out

@@ -1,0 +1,228 @@
+from contextlib import ExitStack
+
+import concourse.mybir as mybir
+
+K, T, E, C, N = 1024, 2048, 4, 256, 512
+SLOTS = E * C
+FLOPS = 2 * K * N * SLOTS
+
+F32 = mybir.dt.float32
+BF16 = mybir.dt.bfloat16
+U32 = mybir.dt.uint32
+U16 = mybir.dt.uint16
+U8 = mybir.dt.uint8
+FP8X4 = mybir.dt.float8_e4m3fn_x4
+
+P = 128
+PACK = 4
+K_PASS = P * PACK
+PASSES = K // K_PASS
+NB = N // P
+HALF = SLOTS // 2
+
+
+def tile_routed_moe_kernel(tc, xT, w, gate, offs, out):
+    nc = tc.nc
+    mult = mybir.AluOpType.mult
+
+    x_view = xT.rearrange("(g p t) n -> g p t n", p=P, t=PACK)
+    w_view = w.rearrange("e (g p j) n -> e g p j n", p=P, j=PACK)
+    gate_view = gate.rearrange("(b p) s -> p b s", p=P)
+
+    with ExitStack() as ctx:
+        held = ctx.enter_context(tc.tile_pool(name="held", bufs=1))
+        stage = ctx.enter_context(tc.tile_pool(name="stage", bufs=10))
+        gpool = ctx.enter_context(tc.tile_pool(name="gathered", bufs=4))
+        xipool = ctx.enter_context(tc.tile_pool(name="xi", bufs=3))
+        wipool = ctx.enter_context(tc.tile_pool(name="wi", bufs=3))
+        ypool = ctx.enter_context(tc.tile_pool(name="ysb", bufs=8))
+        psum = ctx.enter_context(tc.psum_pool(name="psum", bufs=8))
+
+        offsets = held.tile([P, SLOTS // 16], U16, name="offsets")
+        nc.sync.dma_start(offsets[:], offs)
+
+        warm_in = held.tile([P, 8], F32, name="warm_in")
+        warm_out = held.tile([P, 8], F32, name="warm_out")
+        nc.vector.memset(warm_in[:], 0.0)
+        nc.scalar.copy(warm_out[:], warm_in[:])
+
+        planes = {}
+        w_raw = {}
+        gates = {}
+        g4 = {}
+        tok = {}
+        wq = {}
+        ysb = {}
+        windows = []
+
+        def load_plane(i):
+            t = stage.tile([P, T], F32, name="plane%d" % i, tag="stage")
+            nc.sync.dma_start(t[:], x_view[i // PACK, :, i % PACK, :])
+            planes[i] = t
+
+        def load_w(e, g):
+            t = stage.tile([P, PACK, N], F32, name="wraw%d%d" % (e, g), tag="stage")
+            nc.sync.dma_start(t[:], w_view[e, g])
+            w_raw[(e, g)] = t
+
+        def load_gate(e):
+            t = held.tile([P, NB, C], F32, name="gate%d" % e)
+            nc.sync.dma_start(t[:], gate_view[:, :, e * C : (e + 1) * C])
+            gates[e] = t
+
+        def gather(i, c0, c1):
+            g, t = i // PACK, i % PACK
+            h = c0 // HALF
+            if (g, h) not in g4:
+                g4[(g, h)] = gpool.tile([P, PACK, HALF], F32, name="g4_%d%d" % (g, h), tag="g4")
+            nc.vector.tensor_copy(
+                g4[(g, h)][:, t, c0 - h * HALF : c1 - h * HALF],
+                planes[i][:].indirect(offsets[:, c0 // 16 : c1 // 16]),
+            )
+
+        def ileave_tok(g, c0, c1, eng):
+            h = c0 // HALF
+            n = c1 - c0
+            xi = xipool.tile([P, n, PACK], BF16, name="xi%d_%d" % (g, c0), tag="xi", align_bytes=64)
+            src = g4[(g, h)][:, :, c0 - h * HALF : c1 - h * HALF].rearrange("p t n -> p n t")
+            if eng == "s":
+                nc.scalar.copy(xi[:], src)
+            else:
+                nc.vector.tensor_copy(xi[:], src)
+            return xi
+
+        def quant_tok(g, c0, c1, xi):
+            n = c1 - c0
+            codes = held.tile([P, n], U32, name="xq%d_%d" % (g, c0), align_bytes=64)
+            scales = held.tile([P, n], U8, name="xs%d_%d" % (g, c0), align_bytes=64)
+            nc.vector.quantize_mx(
+                out=codes[:].bitcast(FP8X4), scales=scales[:], in_=xi[:].rearrange("p n t -> p (n t)")
+            )
+            for e in range(c0 // C, c1 // C):
+                tok[(g, e)] = (codes, scales, e * C - c0)
+
+        def ileave_w(e, g, eng):
+            wi = wipool.tile([P, N, PACK], BF16, name="wi%d%d" % (e, g), tag="wi", align_bytes=64)
+            src = w_raw[(e, g)][:].rearrange("p j n -> p n j")
+            if eng == "s":
+                nc.scalar.copy(wi[:], src)
+            else:
+                nc.vector.tensor_copy(wi[:], src)
+            return wi
+
+        def quant_w(e, g, wi):
+            codes = held.tile([P, N], U32, name="wq%d%d" % (e, g), align_bytes=64)
+            scales = held.tile([P, N], U8, name="ws%d%d" % (e, g), align_bytes=64)
+            nc.vector.quantize_mx(
+                out=codes[:].bitcast(FP8X4), scales=scales[:], in_=wi[:].rearrange("p n j -> p (n j)")
+            )
+            wq[(e, g)] = (codes, scales)
+
+        def multiply(e, b):
+            acc = psum.tile([P, C], F32, name="acc%d%d" % (e, b), tag="acc")
+            for g in range(PASSES):
+                wc, ws = wq[(e, g)]
+                xc, xs, o = tok[(g, e)]
+                nc.tensor.matmul_mx(
+                    out=acc[:],
+                    lhsT=wc[:, b * P : (b + 1) * P].bitcast(FP8X4),
+                    lhsT_scale=ws[:, b * P : (b + 1) * P],
+                    rhs=xc[:, o : o + C].bitcast(FP8X4),
+                    rhs_scale=xs[:, o : o + C],
+                    start=(g == 0),
+                    stop=(g == PASSES - 1),
+                )
+            y = ypool.tile([P, C], F32, name="y%d%d" % (e, b), tag="y")
+            nc.scalar.copy(y[:], acc[:])
+            ysb[(e, b)] = y
+
+        def scatter(e, b):
+            nc.vector.tensor_tensor(
+                windows[b][:].indirect(offsets[:, e * (C // 16) : (e + 1) * (C // 16)]),
+                ysb[(e, b)][:],
+                gates[e][:, b, :],
+                mult,
+            )
+
+        def store(b):
+            nc.sync.dma_start(out[b * P : (b + 1) * P, :], windows[b][:])
+
+        def prep(e):
+            for g in range(PASSES):
+                quant_w(e, g, ileave_w(e, g, "s"))
+
+        for i in range(6):
+            load_plane(i)
+        load_w(0, 0)
+        load_plane(6)
+        load_plane(7)
+        load_w(0, 1)
+        load_gate(0)
+
+        for t in range(PACK):
+            gather(t, 0, HALF)
+            gather(t, HALF, SLOTS)
+        xi00 = ileave_tok(0, 0, HALF, "s")
+        xi01 = ileave_tok(0, HALF, SLOTS, "s")
+
+        load_w(1, 0)
+        load_w(1, 1)
+        load_gate(1)
+        load_w(2, 0)
+        load_w(2, 1)
+        load_gate(2)
+
+        for i in (4, 5):
+            gather(i, 0, HALF)
+            gather(i, HALF, SLOTS)
+        load_w(3, 0)
+        load_w(3, 1)
+        load_gate(3)
+        quant_tok(0, 0, HALF, xi00)
+        quant_tok(0, HALF, SLOTS, xi01)
+        wi00 = ileave_w(0, 0, "s")
+        gather(6, 0, HALF)
+        gather(6, HALF, SLOTS)
+        quant_w(0, 0, wi00)
+        gather(7, 0, C)
+        xi10 = ileave_tok(1, 0, C, "s")
+        wi01 = ileave_w(0, 1, "s")
+        gather(7, C, HALF)
+        xi11 = ileave_tok(1, C, HALF, "s")
+        gather(7, HALF, SLOTS)
+        xi12 = ileave_tok(1, HALF, SLOTS, "s")
+        quant_tok(1, 0, C, xi10)
+        quant_w(0, 1, wi01)
+        quant_tok(1, C, HALF, xi11)
+        quant_tok(1, HALF, SLOTS, xi12)
+
+        for b in range(NB):
+            win = held.tile([P, T], F32, name="window%d" % b)
+            nc.vector.memset(win[:], 0.0)
+            windows.append(win)
+
+        prep(1)
+        for b in range(NB):
+            multiply(0, b)
+            scatter(0, b)
+        prep(2)
+        for b in range(NB):
+            multiply(1, b)
+            scatter(1, b)
+        prep(3)
+        for b in range(NB):
+            multiply(2, b)
+        scatter(2, 0)
+        scatter(2, 1)
+        for b in range(NB):
+            multiply(3, b)
+        scatter(3, 0)
+        store(0)
+        scatter(2, 2)
+        scatter(3, 1)
+        store(1)
+        scatter(2, 3)
+        scatter(3, 2)
+        store(2)
+        scatter(3, 3)
+        store(3)

@@ -27,6 +27,7 @@ def tile_routed_moe_kernel(tc, xT, w, gate, offs, out):
 
     x_view = xT.rearrange("(g p t) n -> g p t n", p=P, t=PACK)
     w_view = w.rearrange("e (g p j) n -> e g p j n", p=P, j=PACK)
+    NH = N // 2
     gate_view = gate.rearrange("(b p) s -> p b s", p=P)
 
     with ExitStack() as ctx:
@@ -60,10 +61,11 @@ def tile_routed_moe_kernel(tc, xT, w, gate, offs, out):
             nc.sync.dma_start(t[:], x_view[i // PACK, :, i % PACK, :])
             planes[i] = t
 
-        def load_w(e, g):
-            t = stage.tile([P, PACK, N], F32, name="wraw%d%d" % (e, g), tag="stage")
-            nc.sync.dma_start(t[:], w_view[e, g])
-            w_raw[(e, g)] = t
+        def load_wh(e, h):
+            t = stage.tile([P, PASSES, PACK, NH], F32, name="wraw%d%d" % (e, h), tag="stage")
+            for g in range(PASSES):
+                nc.sync.dma_start(t[:, g], w_view[e, g, :, :, h * NH : (h + 1) * NH])
+            w_raw[(e, h)] = t
 
         def load_gate(e):
             t = held.tile([P, NB, C], F32, name="gate%d" % e)
@@ -101,32 +103,33 @@ def tile_routed_moe_kernel(tc, xT, w, gate, offs, out):
             for e in range(c0 // C, c1 // C):
                 tok[(g, e)] = (codes, scales, e * C - c0)
 
-        def ileave_w(e, g, eng):
-            wi = wipool.tile([P, N, PACK], BF16, name="wi%d%d" % (e, g), tag="wi", align_bytes=64)
-            src = w_raw[(e, g)][:].rearrange("p j n -> p n j")
+        def ileave_wh(e, h, eng):
+            wi = wipool.tile([P, PASSES, NH, PACK], BF16, name="wi%d%d" % (e, h), tag="wi", align_bytes=64)
+            src = w_raw[(e, h)][:].rearrange("p g j n -> p g n j")
             if eng == "s":
                 nc.scalar.copy(wi[:], src)
             else:
                 nc.vector.tensor_copy(wi[:], src)
             return wi
 
-        def quant_w(e, g, wi):
-            codes = held.tile([P, N], U32, name="wq%d%d" % (e, g), align_bytes=64)
-            scales = held.tile([P, N], U8, name="ws%d%d" % (e, g), align_bytes=64)
+        def quant_wh(e, h, wi):
+            codes = held.tile([P, PASSES * NH], U32, name="wq%d%d" % (e, h), align_bytes=64)
+            scales = held.tile([P, PASSES * NH], U8, name="ws%d%d" % (e, h), align_bytes=64)
             nc.vector.quantize_mx(
-                out=codes[:].bitcast(FP8X4), scales=scales[:], in_=wi[:].rearrange("p n j -> p (n j)")
+                out=codes[:].bitcast(FP8X4), scales=scales[:], in_=wi[:].rearrange("p g n j -> p (g n j)")
             )
-            wq[(e, g)] = (codes, scales)
+            wq[(e, h)] = (codes, scales)
 
         def multiply(e, b):
             acc = psum.tile([P, C], F32, name="acc%d%d" % (e, b), tag="acc")
+            wc, ws = wq[(e, b // 2)]
             for g in range(PASSES):
-                wc, ws = wq[(e, g)]
                 xc, xs, o = tok[(g, e)]
+                c = g * NH + (b % 2) * P
                 nc.tensor.matmul_mx(
                     out=acc[:],
-                    lhsT=wc[:, b * P : (b + 1) * P].bitcast(FP8X4),
-                    lhsT_scale=ws[:, b * P : (b + 1) * P],
+                    lhsT=wc[:, c : c + P].bitcast(FP8X4),
+                    lhsT_scale=ws[:, c : c + P],
                     rhs=xc[:, o : o + C].bitcast(FP8X4),
                     rhs_scale=xs[:, o : o + C],
                     start=(g == 0),
@@ -147,17 +150,18 @@ def tile_routed_moe_kernel(tc, xT, w, gate, offs, out):
         def store(b):
             nc.sync.dma_start(out[b * P : (b + 1) * P, :], windows[b][:])
 
-        def prep(e):
-            for g in range(PASSES):
-                quant_w(e, g, ileave_w(e, g, "s"))
-
         for i in range(6):
             load_plane(i)
-        load_w(0, 0)
+        load_wh(0, 0)
         load_plane(6)
         load_plane(7)
-        load_w(0, 1)
+        load_wh(0, 1)
         load_gate(0)
+
+        for b in range(NB):
+            win = held.tile([P, T], F32, name="window%d" % b)
+            nc.gpsimd.memset(win[:], 0.0)
+            windows.append(win)
 
         for t in range(PACK):
             gather(t, 0, HALF)
@@ -165,64 +169,54 @@ def tile_routed_moe_kernel(tc, xT, w, gate, offs, out):
         xi00 = ileave_tok(0, 0, HALF, "s")
         xi01 = ileave_tok(0, HALF, SLOTS, "s")
 
-        load_w(1, 0)
-        load_w(1, 1)
+        load_wh(1, 0)
+        load_wh(1, 1)
         load_gate(1)
-        load_w(2, 0)
-        load_w(2, 1)
+        load_wh(2, 0)
         load_gate(2)
+        load_wh(3, 0)
+        load_gate(3)
 
         for i in (4, 5):
             gather(i, 0, HALF)
             gather(i, HALF, SLOTS)
-        load_w(3, 0)
-        load_w(3, 1)
-        load_gate(3)
+        load_wh(2, 1)
+        load_wh(3, 1)
         quant_tok(0, 0, HALF, xi00)
         quant_tok(0, HALF, SLOTS, xi01)
-        wi00 = ileave_w(0, 0, "s")
+        wi0a = ileave_wh(0, 0, "s")
         gather(6, 0, HALF)
         gather(6, HALF, SLOTS)
-        quant_w(0, 0, wi00)
+        quant_wh(0, 0, wi0a)
         gather(7, 0, C)
         xi10 = ileave_tok(1, 0, C, "s")
-        wi01 = ileave_w(0, 1, "s")
         gather(7, C, HALF)
-        xi11 = ileave_tok(1, C, HALF, "s")
         gather(7, HALF, SLOTS)
-        xi12 = ileave_tok(1, HALF, SLOTS, "s")
         quant_tok(1, 0, C, xi10)
-        quant_w(0, 1, wi01)
+        wi0b = ileave_wh(0, 1, "s")
+        xi11 = ileave_tok(1, C, HALF, "v")
+        multiply(0, 0)
+        scatter(0, 0)
+        multiply(0, 1)
+        scatter(0, 1)
+        quant_wh(0, 1, wi0b)
         quant_tok(1, C, HALF, xi11)
+        xi12 = ileave_tok(1, HALF, SLOTS, "v")
         quant_tok(1, HALF, SLOTS, xi12)
-
-        for b in range(NB):
-            win = held.tile([P, T], F32, name="window%d" % b)
-            nc.vector.memset(win[:], 0.0)
-            windows.append(win)
-
-        prep(1)
-        for b in range(NB):
-            multiply(0, b)
-            scatter(0, b)
-        prep(2)
-        for b in range(NB):
-            multiply(1, b)
-            scatter(1, b)
-        prep(3)
-        for b in range(NB):
-            multiply(2, b)
-        scatter(2, 0)
-        scatter(2, 1)
-        for b in range(NB):
-            multiply(3, b)
-        scatter(3, 0)
-        store(0)
-        scatter(2, 2)
-        scatter(3, 1)
-        store(1)
-        scatter(2, 3)
-        scatter(3, 2)
-        store(2)
-        scatter(3, 3)
-        store(3)
+        multiply(0, 2)
+        scatter(0, 2)
+        multiply(0, 3)
+        scatter(0, 3)
+        for h in (0, 1):
+            quant_wh(1, h, ileave_wh(1, h, "s"))
+            for b in (2 * h, 2 * h + 1):
+                multiply(1, b)
+                scatter(1, b)
+        for h in (0, 1):
+            for e in (2, 3):
+                quant_wh(e, h, ileave_wh(e, h, "s"))
+                for b in (2 * h, 2 * h + 1):
+                    multiply(e, b)
+                    scatter(e, b)
+                    if e == 3:
+                        store(b)

@@ -18,7 +18,10 @@ PACK = 4
 K_PASS = P * PACK
 PASSES = K // K_PASS
 NB = N // P
+NH = N // 2
 HALF = SLOTS // 2
+FAST = True
+IT = "svv"
 
 
 def tile_routed_moe_kernel(tc, xT, w, gate, offs, out):
@@ -27,13 +30,11 @@ def tile_routed_moe_kernel(tc, xT, w, gate, offs, out):
 
     x_view = xT.rearrange("(g p t) n -> g p t n", p=P, t=PACK)
     w_view = w.rearrange("e (g p j) n -> e g p j n", p=P, j=PACK)
-    NH = N // 2
     gate_view = gate.rearrange("(b p) s -> p b s", p=P)
 
     with ExitStack() as ctx:
         held = ctx.enter_context(tc.tile_pool(name="held", bufs=1))
         stage = ctx.enter_context(tc.tile_pool(name="stage", bufs=10))
-        gpool = ctx.enter_context(tc.tile_pool(name="gathered", bufs=4))
         xipool = ctx.enter_context(tc.tile_pool(name="xi", bufs=3))
         wipool = ctx.enter_context(tc.tile_pool(name="wi", bufs=3))
         ypool = ctx.enter_context(tc.tile_pool(name="ysb", bufs=8))
@@ -50,11 +51,10 @@ def tile_routed_moe_kernel(tc, xT, w, gate, offs, out):
         planes = {}
         w_raw = {}
         gates = {}
-        g4 = {}
         tok = {}
         wq = {}
-        ysb = {}
         windows = []
+        g4 = [held.tile([P, PACK, SLOTS], F32, name="g4_%d" % g) for g in range(PASSES)]
 
         def load_plane(i):
             t = stage.tile([P, T], F32, name="plane%d" % i, tag="stage")
@@ -62,88 +62,83 @@ def tile_routed_moe_kernel(tc, xT, w, gate, offs, out):
             planes[i] = t
 
         def load_wh(e, h):
-            t = stage.tile([P, PASSES, PACK, NH], F32, name="wraw%d%d" % (e, h), tag="stage")
+            t = stage.tile([P, PACK, PASSES * NH], F32, name="wraw%d%d" % (e, h), tag="stage")
             for g in range(PASSES):
-                nc.sync.dma_start(t[:, g], w_view[e, g, :, :, h * NH : (h + 1) * NH])
+                nc.sync.dma_start(t[:, :, g * NH : (g + 1) * NH], w_view[e, g, :, :, h * NH : (h + 1) * NH])
             w_raw[(e, h)] = t
 
-        def load_gate(e):
-            t = held.tile([P, NB, C], F32, name="gate%d" % e)
-            nc.sync.dma_start(t[:], gate_view[:, :, e * C : (e + 1) * C])
-            gates[e] = t
+        def load_gate(e0, e1):
+            t = held.tile([P, NB, (e1 - e0) * C], F32, name="gate%d" % e0)
+            nc.sync.dma_start(t[:], gate_view[:, :, e0 * C : e1 * C])
+            gates[e0] = t
 
         def gather(i, c0, c1):
-            g, t = i // PACK, i % PACK
-            h = c0 // HALF
-            if (g, h) not in g4:
-                g4[(g, h)] = gpool.tile([P, PACK, HALF], F32, name="g4_%d%d" % (g, h), tag="g4")
             nc.vector.tensor_copy(
-                g4[(g, h)][:, t, c0 - h * HALF : c1 - h * HALF],
+                g4[i // PACK][:, i % PACK, c0:c1],
                 planes[i][:].indirect(offsets[:, c0 // 16 : c1 // 16]),
             )
 
-        def ileave_tok(g, c0, c1, eng):
-            h = c0 // HALF
-            n = c1 - c0
-            xi = xipool.tile([P, n, PACK], BF16, name="xi%d_%d" % (g, c0), tag="xi", align_bytes=64)
-            src = g4[(g, h)][:, :, c0 - h * HALF : c1 - h * HALF].rearrange("p t n -> p n t")
-            if eng == "s":
-                nc.scalar.copy(xi[:], src)
+        def ileave(dst, src, eng):
+            if FAST:
+                o = dst.rearrange("p (c i) t -> p c t i", i=4)
+                s = src.rearrange("p t (c i) -> p c t i", i=4)
             else:
-                nc.vector.tensor_copy(xi[:], src)
-            return xi
+                o = dst
+                s = src.rearrange("p t n -> p n t")
+            if eng == "s":
+                nc.scalar.copy(o, s)
+            else:
+                nc.vector.tensor_copy(o, s)
 
-        def quant_tok(g, c0, c1, xi):
-            n = c1 - c0
-            codes = held.tile([P, n], U32, name="xq%d_%d" % (g, c0), align_bytes=64)
-            scales = held.tile([P, n], U8, name="xs%d_%d" % (g, c0), align_bytes=64)
+        def quant(name, xi, n):
+            codes = held.tile([P, n], U32, name="q" + name, align_bytes=64)
+            scales = held.tile([P, n], U8, name="s" + name, align_bytes=64)
             nc.vector.quantize_mx(
                 out=codes[:].bitcast(FP8X4), scales=scales[:], in_=xi[:].rearrange("p n t -> p (n t)")
             )
+            return codes, scales
+
+        def tok_piece(g, c0, c1, eng):
+            xi = xipool.tile([P, c1 - c0, PACK], BF16, name="xi%d_%d" % (g, c0), tag="xi", align_bytes=64)
+            ileave(xi[:], g4[g][:, :, c0:c1], eng)
+            return xi
+
+        def quant_tok(g, c0, c1, xi):
+            codes, scales = quant("x%d_%d" % (g, c0), xi, c1 - c0)
             for e in range(c0 // C, c1 // C):
                 tok[(g, e)] = (codes, scales, e * C - c0)
 
         def ileave_wh(e, h, eng):
-            wi = wipool.tile([P, PASSES, NH, PACK], BF16, name="wi%d%d" % (e, h), tag="wi", align_bytes=64)
-            src = w_raw[(e, h)][:].rearrange("p g j n -> p g n j")
-            if eng == "s":
-                nc.scalar.copy(wi[:], src)
-            else:
-                nc.vector.tensor_copy(wi[:], src)
+            wi = wipool.tile([P, PASSES * NH, PACK], BF16, name="wi%d%d" % (e, h), tag="wi", align_bytes=64)
+            ileave(wi[:], w_raw[(e, h)][:], eng)
             return wi
 
         def quant_wh(e, h, wi):
-            codes = held.tile([P, PASSES * NH], U32, name="wq%d%d" % (e, h), align_bytes=64)
-            scales = held.tile([P, PASSES * NH], U8, name="ws%d%d" % (e, h), align_bytes=64)
-            nc.vector.quantize_mx(
-                out=codes[:].bitcast(FP8X4), scales=scales[:], in_=wi[:].rearrange("p g n j -> p (g n j)")
-            )
-            wq[(e, h)] = (codes, scales)
+            wq[(e, h)] = quant("w%d%d" % (e, h), wi, PASSES * NH)
 
-        def multiply(e, b):
-            acc = psum.tile([P, C], F32, name="acc%d%d" % (e, b), tag="acc")
-            wc, ws = wq[(e, b // 2)]
-            for g in range(PASSES):
-                xc, xs, o = tok[(g, e)]
-                c = g * NH + (b % 2) * P
-                nc.tensor.matmul_mx(
-                    out=acc[:],
-                    lhsT=wc[:, c : c + P].bitcast(FP8X4),
-                    lhsT_scale=ws[:, c : c + P],
-                    rhs=xc[:, o : o + C].bitcast(FP8X4),
-                    rhs_scale=xs[:, o : o + C],
-                    start=(g == 0),
-                    stop=(g == PASSES - 1),
-                )
-            y = ypool.tile([P, C], F32, name="y%d%d" % (e, b), tag="y")
+        def unit(es, b):
+            n = len(es) * C
+            acc = psum.tile([P, n], F32, name="acc%d%d" % (es[0], b), tag="acc")
+            for k, e in enumerate(es):
+                wc, ws = wq[(e, b // 2)]
+                for g in range(PASSES):
+                    xc, xs, o = tok[(g, e)]
+                    c = g * NH + (b % 2) * P
+                    nc.tensor.matmul_mx(
+                        out=acc[:, k * C : (k + 1) * C],
+                        lhsT=wc[:, c : c + P].bitcast(FP8X4),
+                        lhsT_scale=ws[:, c : c + P],
+                        rhs=xc[:, o : o + C].bitcast(FP8X4),
+                        rhs_scale=xs[:, o : o + C],
+                        start=(g == 0),
+                        stop=(g == PASSES - 1),
+                    )
+            y = ypool.tile([P, n], F32, name="y%d%d" % (es[0], b), tag="y")
             nc.scalar.copy(y[:], acc[:])
-            ysb[(e, b)] = y
-
-        def scatter(e, b):
             nc.vector.tensor_tensor(
-                windows[b][:].indirect(offsets[:, e * (C // 16) : (e + 1) * (C // 16)]),
-                ysb[(e, b)][:],
-                gates[e][:, b, :],
+                windows[b][:].indirect(offsets[:, es[0] * (C // 16) : (es[-1] + 1) * (C // 16)]),
+                y[:],
+                gates[es[0]][:, b, :],
                 mult,
             )
 
@@ -156,7 +151,7 @@ def tile_routed_moe_kernel(tc, xT, w, gate, offs, out):
         load_plane(6)
         load_plane(7)
         load_wh(0, 1)
-        load_gate(0)
+        load_gate(0, 1)
 
         for b in range(NB):
             win = held.tile([P, T], F32, name="window%d" % b)
@@ -166,16 +161,16 @@ def tile_routed_moe_kernel(tc, xT, w, gate, offs, out):
         for t in range(PACK):
             gather(t, 0, HALF)
             gather(t, HALF, SLOTS)
-        xi00 = ileave_tok(0, 0, HALF, "s")
-        xi01 = ileave_tok(0, HALF, SLOTS, "s")
+        xi00 = tok_piece(0, 0, HALF, "s")
+        xi01 = tok_piece(0, HALF, SLOTS, "s")
 
         load_wh(1, 0)
         load_wh(1, 1)
-        load_gate(1)
+        load_gate(1, 2)
         load_wh(2, 0)
-        load_gate(2)
+        load_gate(2, 3)
         load_wh(3, 0)
-        load_gate(3)
+        load_gate(3, 4)
 
         for i in (4, 5):
             gather(i, 0, HALF)
@@ -189,34 +184,28 @@ def tile_routed_moe_kernel(tc, xT, w, gate, offs, out):
         gather(6, HALF, SLOTS)
         quant_wh(0, 0, wi0a)
         gather(7, 0, C)
-        xi10 = ileave_tok(1, 0, C, "s")
+        xi10 = tok_piece(1, 0, C, IT[0])
         gather(7, C, HALF)
         gather(7, HALF, SLOTS)
         quant_tok(1, 0, C, xi10)
         wi0b = ileave_wh(0, 1, "s")
-        xi11 = ileave_tok(1, C, HALF, "v")
-        multiply(0, 0)
-        scatter(0, 0)
-        multiply(0, 1)
-        scatter(0, 1)
+        xi11 = tok_piece(1, C, HALF, IT[1])
+        unit((0,), 0)
+        unit((0,), 1)
         quant_wh(0, 1, wi0b)
         quant_tok(1, C, HALF, xi11)
-        xi12 = ileave_tok(1, HALF, SLOTS, "v")
+        xi12 = tok_piece(1, HALF, SLOTS, IT[2])
         quant_tok(1, HALF, SLOTS, xi12)
-        multiply(0, 2)
-        scatter(0, 2)
-        multiply(0, 3)
-        scatter(0, 3)
+        unit((0,), 2)
+        unit((0,), 3)
         for h in (0, 1):
             quant_wh(1, h, ileave_wh(1, h, "s"))
-            for b in (2 * h, 2 * h + 1):
-                multiply(1, b)
-                scatter(1, b)
+            unit((1,), 2 * h)
+            unit((1,), 2 * h + 1)
         for h in (0, 1):
             for e in (2, 3):
                 quant_wh(e, h, ileave_wh(e, h, "s"))
                 for b in (2 * h, 2 * h + 1):
-                    multiply(e, b)
-                    scatter(e, b)
+                    unit((e,), b)
                     if e == 3:
                         store(b)

@@ -22,6 +22,10 @@ NH = N // 2
 HALF = SLOTS // 2
 FAST = True
 IT = "svv"
+RING = 10
+GRING = False
+SLOT = {}
+LOADS = "p0 p1 p2 p3 p4 p5 w00 p6 p7 w01 g0 w10 w11 g1 w20 g2 w30 g3 w21 w31"
 
 
 def tile_routed_moe_kernel(tc, xT, w, gate, offs, out):
@@ -34,7 +38,8 @@ def tile_routed_moe_kernel(tc, xT, w, gate, offs, out):
 
     with ExitStack() as ctx:
         held = ctx.enter_context(tc.tile_pool(name="held", bufs=1))
-        stage = ctx.enter_context(tc.tile_pool(name="stage", bufs=10))
+        stage = ctx.enter_context(tc.tile_pool(name="stage", bufs=RING))
+        solo = ctx.enter_context(tc.tile_pool(name="solo", bufs=1))
         xipool = ctx.enter_context(tc.tile_pool(name="xi", bufs=3))
         wipool = ctx.enter_context(tc.tile_pool(name="wi", bufs=3))
         ypool = ctx.enter_context(tc.tile_pool(name="ysb", bufs=8))
@@ -57,7 +62,10 @@ def tile_routed_moe_kernel(tc, xT, w, gate, offs, out):
         g4 = [held.tile([P, PACK, SLOTS], F32, name="g4_%d" % g) for g in range(PASSES)]
 
         def load_plane(i):
-            t = stage.tile([P, T], F32, name="plane%d" % i, tag="stage")
+            if i in SLOT.values():
+                t = solo.tile([P, T], F32, name="plane%d" % i, tag="solo%d" % i, align_bytes=64)
+            else:
+                t = stage.tile([P, T], F32, name="plane%d" % i, tag="stage")
             nc.sync.dma_start(t[:], x_view[i // PACK, :, i % PACK, :])
             planes[i] = t
 
@@ -68,7 +76,10 @@ def tile_routed_moe_kernel(tc, xT, w, gate, offs, out):
             w_raw[(e, h)] = t
 
         def load_gate(e0, e1):
-            t = held.tile([P, NB, (e1 - e0) * C], F32, name="gate%d" % e0)
+            if GRING:
+                t = stage.tile([P, NB, (e1 - e0) * C], F32, name="gate%d" % e0, tag="stage")
+            else:
+                t = held.tile([P, NB, (e1 - e0) * C], F32, name="gate%d" % e0)
             nc.sync.dma_start(t[:], gate_view[:, :, e0 * C : e1 * C])
             gates[e0] = t
 
@@ -91,7 +102,10 @@ def tile_routed_moe_kernel(tc, xT, w, gate, offs, out):
                 nc.vector.tensor_copy(o, s)
 
         def quant(name, xi, n):
-            codes = held.tile([P, n], U32, name="q" + name, align_bytes=64)
+            if name in SLOT:
+                codes = solo.tile([P, n], U32, name="q" + name, tag="solo%d" % SLOT[name], align_bytes=64)
+            else:
+                codes = held.tile([P, n], U32, name="q" + name, align_bytes=64)
             scales = held.tile([P, n], U8, name="s" + name, align_bytes=64)
             nc.vector.quantize_mx(
                 out=codes[:].bitcast(FP8X4), scales=scales[:], in_=xi[:].rearrange("p n t -> p (n t)")
@@ -116,14 +130,13 @@ def tile_routed_moe_kernel(tc, xT, w, gate, offs, out):
         def quant_wh(e, h, wi):
             wq[(e, h)] = quant("w%d%d" % (e, h), wi, PASSES * NH)
 
-        def unit(es, b):
-            n = len(es) * C
-            acc = psum.tile([P, n], F32, name="acc%d%d" % (es[0], b), tag="acc")
-            for k, e in enumerate(es):
-                wc, ws = wq[(e, b // 2)]
+        def unit2(e, h):
+            acc = psum.tile([P, 2 * C], F32, name="acc%d%d" % (e, h), tag="acc")
+            wc, ws = wq[(e, h)]
+            for k in range(2):
                 for g in range(PASSES):
                     xc, xs, o = tok[(g, e)]
-                    c = g * NH + (b % 2) * P
+                    c = g * NH + k * P
                     nc.tensor.matmul_mx(
                         out=acc[:, k * C : (k + 1) * C],
                         lhsT=wc[:, c : c + P].bitcast(FP8X4),
@@ -133,25 +146,26 @@ def tile_routed_moe_kernel(tc, xT, w, gate, offs, out):
                         start=(g == 0),
                         stop=(g == PASSES - 1),
                     )
-            y = ypool.tile([P, n], F32, name="y%d%d" % (es[0], b), tag="y")
+            y = ypool.tile([P, 2 * C], F32, name="y%d%d" % (e, h), tag="y")
             nc.scalar.copy(y[:], acc[:])
-            nc.vector.tensor_tensor(
-                windows[b][:].indirect(offsets[:, es[0] * (C // 16) : (es[-1] + 1) * (C // 16)]),
-                y[:],
-                gates[es[0]][:, b, :],
-                mult,
-            )
+            for k in range(2):
+                nc.vector.tensor_tensor(
+                    windows[2 * h + k][:].indirect(offsets[:, e * (C // 16) : (e + 1) * (C // 16)]),
+                    y[:, k * C : (k + 1) * C],
+                    gates[e][:, 2 * h + k, :],
+                    mult,
+                )
 
         def store(b):
             nc.sync.dma_start(out[b * P : (b + 1) * P, :], windows[b][:])
 
-        for i in range(6):
-            load_plane(i)
-        load_wh(0, 0)
-        load_plane(6)
-        load_plane(7)
-        load_wh(0, 1)
-        load_gate(0, 1)
+        for item in LOADS.split():
+            if item[0] == "p":
+                load_plane(int(item[1]))
+            elif item[0] == "w":
+                load_wh(int(item[1]), int(item[2]))
+            else:
+                load_gate(int(item[1]), int(item[1]) + 1)
 
         for b in range(NB):
             win = held.tile([P, T], F32, name="window%d" % b)
@@ -164,19 +178,9 @@ def tile_routed_moe_kernel(tc, xT, w, gate, offs, out):
         xi00 = tok_piece(0, 0, HALF, "s")
         xi01 = tok_piece(0, HALF, SLOTS, "s")
 
-        load_wh(1, 0)
-        load_wh(1, 1)
-        load_gate(1, 2)
-        load_wh(2, 0)
-        load_gate(2, 3)
-        load_wh(3, 0)
-        load_gate(3, 4)
-
         for i in (4, 5):
             gather(i, 0, HALF)
             gather(i, HALF, SLOTS)
-        load_wh(2, 1)
-        load_wh(3, 1)
         quant_tok(0, 0, HALF, xi00)
         quant_tok(0, HALF, SLOTS, xi01)
         wi0a = ileave_wh(0, 0, "s")
@@ -190,22 +194,18 @@ def tile_routed_moe_kernel(tc, xT, w, gate, offs, out):
         quant_tok(1, 0, C, xi10)
         wi0b = ileave_wh(0, 1, "s")
         xi11 = tok_piece(1, C, HALF, IT[1])
-        unit((0,), 0)
-        unit((0,), 1)
+        unit2(0, 0)
         quant_wh(0, 1, wi0b)
         quant_tok(1, C, HALF, xi11)
         xi12 = tok_piece(1, HALF, SLOTS, IT[2])
         quant_tok(1, HALF, SLOTS, xi12)
-        unit((0,), 2)
-        unit((0,), 3)
+        unit2(0, 1)
         for h in (0, 1):
             quant_wh(1, h, ileave_wh(1, h, "s"))
-            unit((1,), 2 * h)
-            unit((1,), 2 * h + 1)
+            unit2(1, h)
         for h in (0, 1):
             for e in (2, 3):
                 quant_wh(e, h, ileave_wh(e, h, "s"))
-                for b in (2 * h, 2 * h + 1):
-                    unit((e,), b)
-                    if e == 3:
-                        store(b)
+                unit2(e, h)
+            store(2 * h)
+            store(2 * h + 1)

@@ -21,7 +21,10 @@ NB = N // P
 NH = N // 2
 HALF = SLOTS // 2
 FAST = True
-IT = "svv"
+IT = "ssv"
+IA = "ss"
+IW = "ssssssss"
+IL = 4
 RING = 10
 GRING = False
 SLOT = {}
@@ -90,14 +93,16 @@ def tile_routed_moe_kernel(tc, xT, w, gate, offs, out):
             )
 
         def ileave(dst, src, eng):
-            if FAST:
-                o = dst.rearrange("p (c i) t -> p c t i", i=4)
-                s = src.rearrange("p t (c i) -> p c t i", i=4)
+            if FAST and eng != "g":
+                o = dst.rearrange("p (c i) t -> p c t i", i=IL)
+                s = src.rearrange("p t (c i) -> p c t i", i=IL)
             else:
                 o = dst
                 s = src.rearrange("p t n -> p n t")
             if eng == "s":
                 nc.scalar.copy(o, s)
+            elif eng == "g":
+                nc.gpsimd.tensor_copy(o, s)
             else:
                 nc.vector.tensor_copy(o, s)
 
@@ -175,15 +180,15 @@ def tile_routed_moe_kernel(tc, xT, w, gate, offs, out):
         for t in range(PACK):
             gather(t, 0, HALF)
             gather(t, HALF, SLOTS)
-        xi00 = tok_piece(0, 0, HALF, "s")
-        xi01 = tok_piece(0, HALF, SLOTS, "s")
+        xi00 = tok_piece(0, 0, HALF, IA[0])
+        xi01 = tok_piece(0, HALF, SLOTS, IA[1])
 
         for i in (4, 5):
             gather(i, 0, HALF)
             gather(i, HALF, SLOTS)
         quant_tok(0, 0, HALF, xi00)
         quant_tok(0, HALF, SLOTS, xi01)
-        wi0a = ileave_wh(0, 0, "s")
+        wi0a = ileave_wh(0, 0, IW[0])
         gather(6, 0, HALF)
         gather(6, HALF, SLOTS)
         quant_wh(0, 0, wi0a)
@@ -192,7 +197,7 @@ def tile_routed_moe_kernel(tc, xT, w, gate, offs, out):
         gather(7, C, HALF)
         gather(7, HALF, SLOTS)
         quant_tok(1, 0, C, xi10)
-        wi0b = ileave_wh(0, 1, "s")
+        wi0b = ileave_wh(0, 1, IW[1])
         xi11 = tok_piece(1, C, HALF, IT[1])
         unit2(0, 0)
         quant_wh(0, 1, wi0b)
@@ -201,11 +206,11 @@ def tile_routed_moe_kernel(tc, xT, w, gate, offs, out):
         quant_tok(1, HALF, SLOTS, xi12)
         unit2(0, 1)
         for h in (0, 1):
-            quant_wh(1, h, ileave_wh(1, h, "s"))
+            quant_wh(1, h, ileave_wh(1, h, IW[2 + h]))
             unit2(1, h)
         for h in (0, 1):
             for e in (2, 3):
-                quant_wh(e, h, ileave_wh(e, h, "s"))
+                quant_wh(e, h, ileave_wh(e, h, IW[2 * e + h]))
                 unit2(e, h)
             store(2 * h)
             store(2 * h + 1)

@@ -24,7 +24,10 @@ FAST = True
 IT = "ssv"
 IA = "ss"
 IW = "ssssssss"
-IL = 4
+IL = 8
+STS = (1, 1, 1, 1)
+MS = "gggg"
+LATE12 = False
 RING = 10
 GRING = False
 SLOT = {}
@@ -118,7 +121,10 @@ def tile_routed_moe_kernel(tc, xT, w, gate, offs, out):
             return codes, scales
 
         def tok_piece(g, c0, c1, eng):
-            xi = xipool.tile([P, c1 - c0, PACK], BF16, name="xi%d_%d" % (g, c0), tag="xi", align_bytes=64)
+            if LATE12 and g == 1 and c0 == HALF:
+                xi = solo.tile([P, c1 - c0, PACK], BF16, name="xi%d_%d" % (g, c0), tag="first", align_bytes=64)
+            else:
+                xi = xipool.tile([P, c1 - c0, PACK], BF16, name="xi%d_%d" % (g, c0), tag="xi", align_bytes=64)
             ileave(xi[:], g4[g][:, :, c0:c1], eng)
             return xi
 
@@ -151,7 +157,10 @@ def tile_routed_moe_kernel(tc, xT, w, gate, offs, out):
                         start=(g == 0),
                         stop=(g == PASSES - 1),
                     )
-            y = ypool.tile([P, 2 * C], F32, name="y%d%d" % (e, h), tag="y")
+            if LATE12 and e == 0 and h == 0:
+                y = solo.tile([P, 2 * C], F32, name="y%d%d" % (e, h), tag="first", align_bytes=64)
+            else:
+                y = ypool.tile([P, 2 * C], F32, name="y%d%d" % (e, h), tag="y")
             nc.scalar.copy(y[:], acc[:])
             for k in range(2):
                 nc.vector.tensor_tensor(
@@ -162,7 +171,9 @@ def tile_routed_moe_kernel(tc, xT, w, gate, offs, out):
                 )
 
         def store(b):
-            nc.sync.dma_start(out[b * P : (b + 1) * P, :], windows[b][:])
+            n = T // STS[b]
+            for k in range(STS[b]):
+                nc.sync.dma_start(out[b * P : (b + 1) * P, k * n : (k + 1) * n], windows[b][:, k * n : (k + 1) * n])
 
         for item in LOADS.split():
             if item[0] == "p":
@@ -174,7 +185,10 @@ def tile_routed_moe_kernel(tc, xT, w, gate, offs, out):
 
         for b in range(NB):
             win = held.tile([P, T], F32, name="window%d" % b)
-            nc.gpsimd.memset(win[:], 0.0)
+            if MS[b] == "g":
+                nc.gpsimd.memset(win[:], 0.0)
+            else:
+                nc.vector.memset(win[:], 0.0)
             windows.append(win)
 
         for t in range(PACK):

@@ -26,7 +26,8 @@ IA = "ss"
 IW = "ssssssss"
 IL = 8
 STS = (1, 1, 1, 1)
-MS = "gggg"
+MS = "vvvv"
+MSREV = False
 LATE12 = False
 RING = 10
 GRING = False
@@ -185,11 +186,12 @@ def tile_routed_moe_kernel(tc, xT, w, gate, offs, out):
 
         for b in range(NB):
             win = held.tile([P, T], F32, name="window%d" % b)
-            if MS[b] == "g":
-                nc.gpsimd.memset(win[:], 0.0)
-            else:
-                nc.vector.memset(win[:], 0.0)
             windows.append(win)
+        for b in (reversed(range(NB)) if MSREV else range(NB)):
+            if MS[b] == "g":
+                nc.gpsimd.memset(windows[b][:], 0.0)
+            else:
+                nc.vector.memset(windows[b][:], 0.0)
 
         for t in range(PACK):
             gather(t, 0, HALF)

@@ -20,19 +20,12 @@ PASSES = K // K_PASS
 NB = N // P
 NH = N // 2
 HALF = SLOTS // 2
-FAST = True
 IT = "ssv"
-IA = "ss"
 IW = "ssssssss"
+RING = 3
 IL = 8
-STS = (1, 1, 1, 1)
-MS = "vvvv"
-MSREV = False
-LATE12 = False
-RING = 10
-GRING = False
-SLOT = {}
-LOADS = "p0 p1 p2 p3 p4 p5 w00 p6 p7 w01 g0 w10 w11 g1 w20 g2 w30 g3 w21 w31"
+SHARED = {"plane0":"b","wraw10":"b","y01":"b","plane1":"d","wraw11":"d","y10":"d","gate1":"c","plane2":"c","wraw20":"f","y11":"f","plane3":"f","wraw30":"g","y20":"g","plane4":"g","gate2":"h","plane5":"h","plane7":"e","wraw31":"e","y30":"e"}
+LOADS = "p0 p1 p2 p3 p4 p5 p6 w00 p7 g01 w01 w10 w11 g12 w20 w30 w21 g24 w31"
 
 
 def tile_routed_moe_kernel(tc, xT, w, gate, offs, out):
@@ -49,7 +42,7 @@ def tile_routed_moe_kernel(tc, xT, w, gate, offs, out):
         solo = ctx.enter_context(tc.tile_pool(name="solo", bufs=1))
         xipool = ctx.enter_context(tc.tile_pool(name="xi", bufs=3))
         wipool = ctx.enter_context(tc.tile_pool(name="wi", bufs=3))
-        ypool = ctx.enter_context(tc.tile_pool(name="ysb", bufs=8))
+        ypool = ctx.enter_context(tc.tile_pool(name="ysb", bufs=6))
         psum = ctx.enter_context(tc.psum_pool(name="psum", bufs=8))
 
         offsets = held.tile([P, SLOTS // 16], U16, name="offsets")
@@ -66,55 +59,56 @@ def tile_routed_moe_kernel(tc, xT, w, gate, offs, out):
         tok = {}
         wq = {}
         windows = []
-        g4 = [held.tile([P, PACK, SLOTS], F32, name="g4_%d" % g) for g in range(PASSES)]
+        def tile_of(pool, shape, dtype, name, tag):
+            if name in SHARED:
+                return solo.tile(shape, dtype, name=name, tag="shared_" + SHARED[name], align_bytes=64)
+            return pool.tile(shape, dtype, name=name, tag=tag, align_bytes=64)
+
+        g4 = {}
+        g4[(0, 0)] = held.tile([P, PACK, HALF], F32, name="g0a")
+        g4[(0, HALF)] = tile_of(held, [P, 2, HALF], F32, "g0b", "g0b")
+        g4[(1, 0)] = held.tile([P, PACK, HALF], F32, name="g1a")
+        g4[(1, HALF)] = held.tile([P, PACK, HALF], F32, name="g1b")
+        half = [tile_of(held, [P, T], BF16, "half%d" % i, "half%d" % i) for i in range(2)]
+        ahead = xipool.tile([P, HALF, PACK], BF16, name="xi0_512", tag="xi", align_bytes=64)
 
         def load_plane(i):
-            if i in SLOT.values():
-                t = solo.tile([P, T], F32, name="plane%d" % i, tag="solo%d" % i, align_bytes=64)
-            else:
-                t = stage.tile([P, T], F32, name="plane%d" % i, tag="stage")
+            t = tile_of(stage, [P, T], F32, "plane%d" % i, "stage")
             nc.sync.dma_start(t[:], x_view[i // PACK, :, i % PACK, :])
             planes[i] = t
 
         def load_wh(e, h):
-            t = stage.tile([P, PACK, PASSES * NH], F32, name="wraw%d%d" % (e, h), tag="stage")
+            t = tile_of(stage, [P, PACK, PASSES * NH], F32, "wraw%d%d" % (e, h), "stage")
             for g in range(PASSES):
                 nc.sync.dma_start(t[:, :, g * NH : (g + 1) * NH], w_view[e, g, :, :, h * NH : (h + 1) * NH])
             w_raw[(e, h)] = t
 
         def load_gate(e0, e1):
-            if GRING:
-                t = stage.tile([P, NB, (e1 - e0) * C], F32, name="gate%d" % e0, tag="stage")
-            else:
-                t = held.tile([P, NB, (e1 - e0) * C], F32, name="gate%d" % e0)
+            t = tile_of(held, [P, NB, (e1 - e0) * C], F32, "gate%d" % e0, "gate%d" % e0)
             nc.sync.dma_start(t[:], gate_view[:, :, e0 * C : e1 * C])
-            gates[e0] = t
+            for e in range(e0, e1):
+                gates[e] = t[:, :, (e - e0) * C : (e - e0 + 1) * C]
+            gates[(e0, e1)] = t
 
         def gather(i, c0, c1):
+            h0 = c0 // HALF * HALF
+            dst = g4[(i // PACK, h0)]
+            row = i % PACK + dst.shape[1] - PACK
             nc.vector.tensor_copy(
-                g4[i // PACK][:, i % PACK, c0:c1],
+                dst[:, row, c0 - h0 : c1 - h0],
                 planes[i][:].indirect(offsets[:, c0 // 16 : c1 // 16]),
             )
 
         def ileave(dst, src, eng):
-            if FAST and eng != "g":
-                o = dst.rearrange("p (c i) t -> p c t i", i=IL)
-                s = src.rearrange("p t (c i) -> p c t i", i=IL)
-            else:
-                o = dst
-                s = src.rearrange("p t n -> p n t")
+            o = dst.rearrange("p (c i) t -> p c t i", i=IL)
+            s = src.rearrange("p t (c i) -> p c t i", i=IL)
             if eng == "s":
                 nc.scalar.copy(o, s)
-            elif eng == "g":
-                nc.gpsimd.tensor_copy(o, s)
             else:
                 nc.vector.tensor_copy(o, s)
 
         def quant(name, xi, n):
-            if name in SLOT:
-                codes = solo.tile([P, n], U32, name="q" + name, tag="solo%d" % SLOT[name], align_bytes=64)
-            else:
-                codes = held.tile([P, n], U32, name="q" + name, align_bytes=64)
+            codes = tile_of(held, [P, n], U32, "q" + name, "q" + name)
             scales = held.tile([P, n], U8, name="s" + name, align_bytes=64)
             nc.vector.quantize_mx(
                 out=codes[:].bitcast(FP8X4), scales=scales[:], in_=xi[:].rearrange("p n t -> p (n t)")
@@ -122,11 +116,9 @@ def tile_routed_moe_kernel(tc, xT, w, gate, offs, out):
             return codes, scales
 
         def tok_piece(g, c0, c1, eng):
-            if LATE12 and g == 1 and c0 == HALF:
-                xi = solo.tile([P, c1 - c0, PACK], BF16, name="xi%d_%d" % (g, c0), tag="first", align_bytes=64)
-            else:
-                xi = xipool.tile([P, c1 - c0, PACK], BF16, name="xi%d_%d" % (g, c0), tag="xi", align_bytes=64)
-            ileave(xi[:], g4[g][:, :, c0:c1], eng)
+            xi = tile_of(xipool, [P, c1 - c0, PACK], BF16, "xi%d_%d" % (g, c0), "xi")
+            h0 = c0 // HALF * HALF
+            ileave(xi[:], g4[(g, h0)][:, :, c0 - h0 : c1 - h0], eng)
             return xi
 
         def quant_tok(g, c0, c1, xi):
@@ -135,7 +127,7 @@ def tile_routed_moe_kernel(tc, xT, w, gate, offs, out):
                 tok[(g, e)] = (codes, scales, e * C - c0)
 
         def ileave_wh(e, h, eng):
-            wi = wipool.tile([P, PASSES * NH, PACK], BF16, name="wi%d%d" % (e, h), tag="wi", align_bytes=64)
+            wi = tile_of(wipool, [P, PASSES * NH, PACK], BF16, "wi%d%d" % (e, h), "wi")
             ileave(wi[:], w_raw[(e, h)][:], eng)
             return wi
 
@@ -158,10 +150,7 @@ def tile_routed_moe_kernel(tc, xT, w, gate, offs, out):
                         start=(g == 0),
                         stop=(g == PASSES - 1),
                     )
-            if LATE12 and e == 0 and h == 0:
-                y = solo.tile([P, 2 * C], F32, name="y%d%d" % (e, h), tag="first", align_bytes=64)
-            else:
-                y = ypool.tile([P, 2 * C], F32, name="y%d%d" % (e, h), tag="y")
+            y = tile_of(ypool, [P, 2 * C], F32, "y%d%d" % (e, h), "y")
             nc.scalar.copy(y[:], acc[:])
             for k in range(2):
                 nc.vector.tensor_tensor(
@@ -171,10 +160,33 @@ def tile_routed_moe_kernel(tc, xT, w, gate, offs, out):
                     mult,
                 )
 
+        def block_unit(k):
+            acc = psum.tile([P, 2 * C], F32, name="accb%d" % k, tag="acc")
+            for j, e in enumerate((2, 3)):
+                wc, ws = wq[(e, 1)]
+                for g in range(PASSES):
+                    xc, xs, o = tok[(g, e)]
+                    c = g * NH + k * P
+                    nc.tensor.matmul_mx(
+                        out=acc[:, j * C : (j + 1) * C],
+                        lhsT=wc[:, c : c + P].bitcast(FP8X4),
+                        lhsT_scale=ws[:, c : c + P],
+                        rhs=xc[:, o : o + C].bitcast(FP8X4),
+                        rhs_scale=xs[:, o : o + C],
+                        start=(g == 0),
+                        stop=(g == PASSES - 1),
+                    )
+            y = tile_of(ypool, [P, 2 * C], F32, "yb%d" % k, "y")
+            nc.scalar.copy(y[:], acc[:])
+            nc.vector.tensor_tensor(
+                windows[2 + k][:].indirect(offsets[:, HALF // 16 :]),
+                y[:],
+                gates[(2, 4)][:, 2 + k, :],
+                mult,
+            )
+
         def store(b):
-            n = T // STS[b]
-            for k in range(STS[b]):
-                nc.sync.dma_start(out[b * P : (b + 1) * P, k * n : (k + 1) * n], windows[b][:, k * n : (k + 1) * n])
+            nc.sync.dma_start(out[b * P : (b + 1) * P, :], windows[b][:])
 
         for item in LOADS.split():
             if item[0] == "p":
@@ -182,22 +194,25 @@ def tile_routed_moe_kernel(tc, xT, w, gate, offs, out):
             elif item[0] == "w":
                 load_wh(int(item[1]), int(item[2]))
             else:
-                load_gate(int(item[1]), int(item[1]) + 1)
+                load_gate(int(item[1]), int(item[2]))
 
         for b in range(NB):
             win = held.tile([P, T], F32, name="window%d" % b)
             windows.append(win)
-        for b in (reversed(range(NB)) if MSREV else range(NB)):
-            if MS[b] == "g":
-                nc.gpsimd.memset(windows[b][:], 0.0)
-            else:
-                nc.vector.memset(windows[b][:], 0.0)
+            nc.vector.memset(win[:], 0.0)
 
-        for t in range(PACK):
+        for t in (0, 1):
+            gather(t, 0, HALF)
+            nc.scalar.copy(half[t][:], planes[t][:])
+            nc.scalar.activation(
+                ahead[:, :, t], half[t][:].indirect(offsets[:, HALF // 16 :]), mybir.ActivationFunctionType.Copy
+            )
+        for t in (2, 3):
             gather(t, 0, HALF)
             gather(t, HALF, SLOTS)
-        xi00 = tok_piece(0, 0, HALF, IA[0])
-        xi01 = tok_piece(0, HALF, SLOTS, IA[1])
+        xi00 = tok_piece(0, 0, HALF, "s")
+        ileave(ahead[:, :, 2:4], g4[(0, HALF)][:], "s")
+        xi01 = ahead
 
         for i in (4, 5):
             gather(i, 0, HALF)
@@ -224,9 +239,14 @@ def tile_routed_moe_kernel(tc, xT, w, gate, offs, out):
         for h in (0, 1):
             quant_wh(1, h, ileave_wh(1, h, IW[2 + h]))
             unit2(1, h)
-        for h in (0, 1):
-            for e in (2, 3):
-                quant_wh(e, h, ileave_wh(e, h, IW[2 * e + h]))
-                unit2(e, h)
-            store(2 * h)
-            store(2 * h + 1)
+        quant_wh(2, 0, ileave_wh(2, 0, IW[4]))
+        unit2(2, 0)
+        quant_wh(3, 0, ileave_wh(3, 0, IW[6]))
+        for e in (2, 3):
+            quant_wh(e, 1, ileave_wh(e, 1, IW[2 * e + 1]))
+        unit2(3, 0)
+        store(0)
+        store(1)
+        for k in (0, 1):
+            block_unit(k)
+            store(2 + k)

@@ -46,7 +46,6 @@ def tile_routed_moe_kernel(tc, xT, w, gate, offs, out):
         psum = ctx.enter_context(tc.psum_pool(name="psum", bufs=8))
 
         offsets = held.tile([P, SLOTS // 16], U16, name="offsets")
-        nc.sync.dma_start(offsets[:], offs)
 
         warm_in = held.tile([P, 8], F32, name="warm_in")
         warm_out = held.tile([P, 8], F32, name="warm_out")
@@ -191,6 +190,8 @@ def tile_routed_moe_kernel(tc, xT, w, gate, offs, out):
         for item in LOADS.split():
             if item[0] == "p":
                 load_plane(int(item[1]))
+                if item[1] == "0":
+                    nc.sync.dma_start(offsets[:], offs)
             elif item[0] == "w":
                 load_wh(int(item[1]), int(item[2]))
             else:

from contextlib import ExitStack

import concourse.mybir as mybir

K, T, E, C, N = 1024, 2048, 4, 256, 512
SLOTS = E * C
FLOPS = 2 * K * N * SLOTS

F32 = mybir.dt.float32
BF16 = mybir.dt.bfloat16
U32 = mybir.dt.uint32
U16 = mybir.dt.uint16
U8 = mybir.dt.uint8
FP8X4 = mybir.dt.float8_e4m3fn_x4

P = 128
PACK = 4
K_PASS = P * PACK
PASSES = K // K_PASS
NB = N // P
NH = N // 2
HALF = SLOTS // 2
IT = "ssv"
IW = "ssssssss"
RING = 3
IL = 8
SHARED = {"plane0":"b","wraw10":"b","y01":"b","plane1":"d","wraw11":"d","y10":"d","gate1":"c","plane2":"c","wraw20":"f","y11":"f","plane3":"f","wraw30":"g","y20":"g","plane4":"g","gate2":"h","plane5":"h","plane7":"e","wraw31":"e","y30":"e"}
LOADS = "p0 p1 p2 p3 p4 p5 p6 w00 p7 g01 w01 w10 w11 g12 w20 w30 w21 g24 w31"


def tile_routed_moe_kernel(tc, xT, w, gate, offs, out):
    nc = tc.nc
    mult = mybir.AluOpType.mult

    x_view = xT.rearrange("(g p t) n -> g p t n", p=P, t=PACK)
    w_view = w.rearrange("e (g p j) n -> e g p j n", p=P, j=PACK)
    gate_view = gate.rearrange("(b p) s -> p b s", p=P)

    with ExitStack() as ctx:
        held = ctx.enter_context(tc.tile_pool(name="held", bufs=1))
        stage = ctx.enter_context(tc.tile_pool(name="stage", bufs=RING))
        solo = ctx.enter_context(tc.tile_pool(name="solo", bufs=1))
        xipool = ctx.enter_context(tc.tile_pool(name="xi", bufs=3))
        wipool = ctx.enter_context(tc.tile_pool(name="wi", bufs=3))
        ypool = ctx.enter_context(tc.tile_pool(name="ysb", bufs=6))
        psum = ctx.enter_context(tc.psum_pool(name="psum", bufs=8))

        offsets = held.tile([P, SLOTS // 16], U16, name="offsets")

        warm_in = held.tile([P, 8], F32, name="warm_in")
        warm_out = held.tile([P, 8], F32, name="warm_out")
        nc.vector.memset(warm_in[:], 0.0)
        nc.scalar.copy(warm_out[:], warm_in[:])

        planes = {}
        w_raw = {}
        gates = {}
        tok = {}
        wq = {}
        windows = []
        def tile_of(pool, shape, dtype, name, tag):
            if name in SHARED:
                return solo.tile(shape, dtype, name=name, tag="shared_" + SHARED[name], align_bytes=64)
            return pool.tile(shape, dtype, name=name, tag=tag, align_bytes=64)

        g4 = {}
        g4[(0, 0)] = held.tile([P, PACK, HALF], F32, name="g0a")
        g4[(0, HALF)] = tile_of(held, [P, 2, HALF], F32, "g0b", "g0b")
        g4[(1, 0)] = held.tile([P, PACK, HALF], F32, name="g1a")
        g4[(1, HALF)] = held.tile([P, PACK, HALF], F32, name="g1b")
        half = [tile_of(held, [P, T], BF16, "half%d" % i, "half%d" % i) for i in range(2)]
        ahead = xipool.tile([P, HALF, PACK], BF16, name="xi0_512", tag="xi", align_bytes=64)

        def load_plane(i):
            t = tile_of(stage, [P, T], F32, "plane%d" % i, "stage")
            nc.sync.dma_start(t[:], x_view[i // PACK, :, i % PACK, :])
            planes[i] = t

        def load_wh(e, h):
            t = tile_of(stage, [P, PACK, PASSES * NH], F32, "wraw%d%d" % (e, h), "stage")
            for g in range(PASSES):
                nc.sync.dma_start(t[:, :, g * NH : (g + 1) * NH], w_view[e, g, :, :, h * NH : (h + 1) * NH])
            w_raw[(e, h)] = t

        def load_gate(e0, e1):
            t = tile_of(held, [P, NB, (e1 - e0) * C], F32, "gate%d" % e0, "gate%d" % e0)
            nc.sync.dma_start(t[:], gate_view[:, :, e0 * C : e1 * C])
            for e in range(e0, e1):
                gates[e] = t[:, :, (e - e0) * C : (e - e0 + 1) * C]
            gates[(e0, e1)] = t

        def gather(i, c0, c1):
            h0 = c0 // HALF * HALF
            dst = g4[(i // PACK, h0)]
            row = i % PACK + dst.shape[1] - PACK
            nc.vector.tensor_copy(
                dst[:, row, c0 - h0 : c1 - h0],
                planes[i][:].indirect(offsets[:, c0 // 16 : c1 // 16]),
            )

        def ileave(dst, src, eng):
            o = dst.rearrange("p (c i) t -> p c t i", i=IL)
            s = src.rearrange("p t (c i) -> p c t i", i=IL)
            if eng == "s":
                nc.scalar.copy(o, s)
            else:
                nc.vector.tensor_copy(o, s)

        def quant(name, xi, n):
            codes = tile_of(held, [P, n], U32, "q" + name, "q" + name)
            scales = held.tile([P, n], U8, name="s" + name, align_bytes=64)
            nc.vector.quantize_mx(
                out=codes[:].bitcast(FP8X4), scales=scales[:], in_=xi[:].rearrange("p n t -> p (n t)")
            )
            return codes, scales

        def tok_piece(g, c0, c1, eng):
            xi = tile_of(xipool, [P, c1 - c0, PACK], BF16, "xi%d_%d" % (g, c0), "xi")
            h0 = c0 // HALF * HALF
            ileave(xi[:], g4[(g, h0)][:, :, c0 - h0 : c1 - h0], eng)
            return xi

        def quant_tok(g, c0, c1, xi):
            codes, scales = quant("x%d_%d" % (g, c0), xi, c1 - c0)
            for e in range(c0 // C, c1 // C):
                tok[(g, e)] = (codes, scales, e * C - c0)

        def ileave_wh(e, h, eng):
            wi = tile_of(wipool, [P, PASSES * NH, PACK], BF16, "wi%d%d" % (e, h), "wi")
            ileave(wi[:], w_raw[(e, h)][:], eng)
            return wi

        def quant_wh(e, h, wi):
            wq[(e, h)] = quant("w%d%d" % (e, h), wi, PASSES * NH)

        def unit2(e, h):
            acc = psum.tile([P, 2 * C], F32, name="acc%d%d" % (e, h), tag="acc")
            wc, ws = wq[(e, h)]
            for k in range(2):
                for g in range(PASSES):
                    xc, xs, o = tok[(g, e)]
                    c = g * NH + k * P
                    nc.tensor.matmul_mx(
                        out=acc[:, k * C : (k + 1) * C],
                        lhsT=wc[:, c : c + P].bitcast(FP8X4),
                        lhsT_scale=ws[:, c : c + P],
                        rhs=xc[:, o : o + C].bitcast(FP8X4),
                        rhs_scale=xs[:, o : o + C],
                        start=(g == 0),
                        stop=(g == PASSES - 1),
                    )
            y = tile_of(ypool, [P, 2 * C], F32, "y%d%d" % (e, h), "y")
            nc.scalar.copy(y[:], acc[:])
            for k in range(2):
                nc.vector.tensor_tensor(
                    windows[2 * h + k][:].indirect(offsets[:, e * (C // 16) : (e + 1) * (C // 16)]),
                    y[:, k * C : (k + 1) * C],
                    gates[e][:, 2 * h + k, :],
                    mult,
                )

        def block_unit(k):
            acc = psum.tile([P, 2 * C], F32, name="accb%d" % k, tag="acc")
            for j, e in enumerate((2, 3)):
                wc, ws = wq[(e, 1)]
                for g in range(PASSES):
                    xc, xs, o = tok[(g, e)]
                    c = g * NH + k * P
                    nc.tensor.matmul_mx(
                        out=acc[:, j * C : (j + 1) * C],
                        lhsT=wc[:, c : c + P].bitcast(FP8X4),
                        lhsT_scale=ws[:, c : c + P],
                        rhs=xc[:, o : o + C].bitcast(FP8X4),
                        rhs_scale=xs[:, o : o + C],
                        start=(g == 0),
                        stop=(g == PASSES - 1),
                    )
            y = tile_of(ypool, [P, 2 * C], F32, "yb%d" % k, "y")
            nc.scalar.copy(y[:], acc[:])
            nc.vector.tensor_tensor(
                windows[2 + k][:].indirect(offsets[:, HALF // 16 :]),
                y[:],
                gates[(2, 4)][:, 2 + k, :],
                mult,
            )

        def store(b):
            nc.sync.dma_start(out[b * P : (b + 1) * P, :], windows[b][:])

        for item in LOADS.split():
            if item[0] == "p":
                load_plane(int(item[1]))
                if item[1] == "0":
                    nc.sync.dma_start(offsets[:], offs)
            elif item[0] == "w":
                load_wh(int(item[1]), int(item[2]))
            else:
                load_gate(int(item[1]), int(item[2]))

        for b in range(NB):
            win = held.tile([P, T], F32, name="window%d" % b)
            windows.append(win)
            nc.vector.memset(win[:], 0.0)

        for t in (0, 1):
            gather(t, 0, HALF)
            nc.scalar.copy(half[t][:], planes[t][:])
            nc.scalar.activation(
                ahead[:, :, t], half[t][:].indirect(offsets[:, HALF // 16 :]), mybir.ActivationFunctionType.Copy
            )
        for t in (2, 3):
            gather(t, 0, HALF)
            gather(t, HALF, SLOTS)
        xi00 = tok_piece(0, 0, HALF, "s")
        ileave(ahead[:, :, 2:4], g4[(0, HALF)][:], "s")
        xi01 = ahead

        for i in (4, 5):
            gather(i, 0, HALF)
            gather(i, HALF, SLOTS)
        quant_tok(0, 0, HALF, xi00)
        quant_tok(0, HALF, SLOTS, xi01)
        wi0a = ileave_wh(0, 0, IW[0])
        gather(6, 0, HALF)
        gather(6, HALF, SLOTS)
        quant_wh(0, 0, wi0a)
        gather(7, 0, C)
        xi10 = tok_piece(1, 0, C, IT[0])
        gather(7, C, HALF)
        gather(7, HALF, SLOTS)
        quant_tok(1, 0, C, xi10)
        wi0b = ileave_wh(0, 1, IW[1])
        xi11 = tok_piece(1, C, HALF, IT[1])
        unit2(0, 0)
        quant_wh(0, 1, wi0b)
        quant_tok(1, C, HALF, xi11)
        xi12 = tok_piece(1, HALF, SLOTS, IT[2])
        quant_tok(1, HALF, SLOTS, xi12)
        unit2(0, 1)
        for h in (0, 1):
            quant_wh(1, h, ileave_wh(1, h, IW[2 + h]))
            unit2(1, h)
        quant_wh(2, 0, ileave_wh(2, 0, IW[4]))
        unit2(2, 0)
        quant_wh(3, 0, ileave_wh(3, 0, IW[6]))
        for e in (2, 3):
            quant_wh(e, 1, ileave_wh(e, 1, IW[2 * e + 1]))
        unit2(3, 0)
        store(0)
        store(1)
        for k in (0, 1):
            block_unit(k)
            store(2 + k)
